import numpy as np
import ml_dtypes


def mxq(x, axis, fmt="e4m3"):
    dtype, down = {"e4m3": (ml_dtypes.float8_e4m3fn, 7), "e5m2": (ml_dtypes.float8_e5m2, 14)}[fmt]
    v = np.moveaxis(np.asarray(x, np.float32).astype(ml_dtypes.bfloat16).astype(np.float64), axis, -1)
    blocks = v.reshape(v.shape[:-1] + (-1, 32))
    amax = np.abs(blocks).max(-1, keepdims=True)
    byte = np.maximum(np.where(amax > 0, np.frexp(amax)[1] - 1 + 127, 0) - down, 1)
    scale = np.exp2(byte - 127.0)
    codes = (blocks / scale).astype(np.float32).astype(dtype).astype(np.float64)
    return np.moveaxis((codes * scale).reshape(v.shape), -1, axis)


WIDE = False


def mx_kscale(k):
    if not WIDE:
        return np.ones(k)
    levels = np.array([10, -10, 5, -5, 0])
    if k % 512:
        return np.exp2(np.random.permutation(np.resize(levels, k // 32))).repeat(32)
    a = np.empty((k // 512, 16))
    for p in range(k // 512):
        a[p, :8] = np.random.permutation(np.resize(levels, 8))
        for g in range(8):
            far = levels[np.abs(levels - a[p, g]) >= 10]
            a[p, g + 8] = far[np.random.randint(len(far))]
    return np.exp2(a.ravel()).repeat(32)


def f64(x):
    return np.asarray(x).astype(np.float64)


def striped(idx):
    return np.tile(idx.reshape(-1, 16).T, (8, 1)).astype(np.uint16)


def unstriped(offs):
    return offs[:16].T.reshape(-1).astype(np.int64)


E2M1 = np.array([0.0, 0.5, 1.0, 1.5, 2.0, 3.0, 4.0, 6.0, -0.0, -0.5, -1.0, -1.5, -2.0, -3.0, -4.0, -6.0])


def pack_weight(w, fmt):
    k, n = w.shape
    w = f64(np.asarray(w, np.float32).astype(ml_dtypes.bfloat16)).reshape(k // 32, 32, n)
    amax = np.abs(w).max(1)
    if fmt == "e4m3":
        byte = np.frexp(amax)[1] - 1 + 127 - 7
    else:
        mant, ex = np.frexp(amax / 6.0)
        byte = np.where(mant > 0.5, ex, ex - 1) + 127
    byte = np.clip(np.where(amax > 0, byte, 1), 1, 254)
    scaled = (w * np.exp2(127.0 - byte)[:, None, :]).reshape(k, n).astype(np.float32)
    by_word = np.ascontiguousarray(scaled.reshape(k // 512, 128, 4, n).transpose(0, 1, 3, 2))
    if fmt == "e4m3":
        words = by_word.astype(ml_dtypes.float8_e4m3fn).view(np.uint8)
    else:
        c = by_word.astype(ml_dtypes.float4_e2m1fn).view(np.uint8) & 0xF
        words = (c[..., 0::2] | (c[..., 1::2] << 4)).reshape(k // 512, 128, 2 * n)
    return np.ascontiguousarray(words), np.ascontiguousarray(byte.astype(np.uint8).reshape(k // 512, 16, n))


def unpack_weight(words, scales, fmt):
    g, _, n = scales.shape
    words = np.ascontiguousarray(words).reshape(g, 128, n, -1)
    if fmt == "e4m3":
        vals = words.view(ml_dtypes.float8_e4m3fn).astype(np.float64)
    else:
        nib = np.empty((g, 128, n, 4), np.uint8)
        nib[..., 0::2] = words & 0xF
        nib[..., 1::2] = words >> 4
        vals = E2M1[nib]
    vals = vals * np.repeat(np.exp2(scales.astype(np.float64) - 127.0), 8, axis=1)[..., None]
    return vals.transpose(0, 1, 3, 2).reshape(g * 512, n)


def gelu(v):
    return 0.5 * v * (1.0 + np.tanh(np.sqrt(2.0 / np.pi) * (v + 0.044715 * v**3)))


K, T, S, P, M, H, N = 1024, 2048, 1024, 512, 512, 1024, 512


def setup_inputs():
    n = np.random.standard_normal
    f32 = np.float32
    s = mx_kscale(K)[:, None]
    um = mx_kscale(M)
    u = mx_kscale(H)
    perm = np.random.permutation(S)
    tab_words, tab_scales = pack_weight(n((K, T)) * s, "e4m3")
    w1_words, w1_scales = pack_weight(n((K, M)) / np.sqrt(K) / s, "e2m1")
    w4_words, w4_scales = pack_weight(n((H, N)) / np.sqrt(H) / u[:, None], "e4m3")
    return {
        "tab_words": tab_words, "tab_scales": tab_scales,
        "offs": striped(np.random.permutation(T)[:S]),
        "pos1": striped(perm[:P]),
        "pos2": striped(perm[P:]),
        "w1_words": w1_words, "w1_scales": w1_scales,
        "w2": (n((K, M)) / np.sqrt(K) / s).astype(f32),
        "gain": (np.random.uniform(0.5, 1.5, M) * um).astype(f32),
        "w3": (0.8 * n((M, H)) / np.sqrt(M) / um[:, None]).astype(f32),
        "slope": np.random.uniform(0.6, 3.0, H).astype(f32),
        "thr": n(H).astype(f32),
        "tint": (1.5 * n((H, P))).astype(f32),
        "shade0": (0.6 * n(H)).astype(f32),
        "wgs": np.exp(0.3 * n((128, P))).astype(f32),
        "gain2": (np.random.uniform(0.5, 1.5, H) * u).astype(f32),
        "w4_words": w4_words, "w4_scales": w4_scales,
        "tone": np.exp(0.4 * n(N)).astype(f32),
    }


def reference(tab_words, tab_scales, offs, pos1, pos2, w1_words, w1_scales, w2, gain, w3,
              slope, thr, tint, shade0, wgs, gain2, w4_words, w4_scales, tone):
    v = unpack_weight(tab_words, tab_scales, "e4m3")[:, unstriped(offs)]
    e1 = unpack_weight(w1_words, w1_scales, "e2m1").T @ v
    e2 = mxq(f64(w2), 0, "e4m3").T @ v
    e = mxq(np.maximum(e1, e2) * f64(gain)[:, None], 0, "e4m3")
    h = mxq(f64(w3), 0, "e4m3").T @ e
    a = 1.0 / (1.0 + np.exp(-(f64(slope)[:, None] * h[:, unstriped(pos1)] + f64(thr)[:, None])))
    a = a * f64(tint)
    page = h + f64(shade0)[:, None]
    page[:, unstriped(pos2)] = np.tile(f64(wgs), (H // 128, 1)) * a
    y = mxq(page * f64(gain2)[:, None], 0, "e4m3")
    return f64(tone)[:, None] * (unpack_weight(w4_words, w4_scales, "e4m3").T @ y)

@@ -1,0 +1,292 @@
+from contextlib import ExitStack
+
+import concourse.mybir as mybir
+
+K, T, S, LOOKS, M, H, N = 1024, 2048, 1024, 512, 512, 1024, 512
+FLOPS = 2 * (2 * K * M * S + M * H * S + H * N * S)
+
+F32 = mybir.dt.float32
+BF16 = mybir.dt.bfloat16
+I32 = mybir.dt.int32
+U32 = mybir.dt.uint32
+U16 = mybir.dt.uint16
+U8 = mybir.dt.uint8
+FP8X4 = mybir.dt.float8_e4m3fn_x4
+FP4X4 = mybir.dt.float4_e2m1fn_x4
+ACT = mybir.ActivationFunctionType
+ALU = mybir.AluOpType
+
+P = 128
+PACK = 4
+KP = P * PACK
+HALF = 512
+
+
+def tile_list_indigo_shade_readout_kernel(
+    tc, tab_words, tab_scales, offs, pos1, pos2, w1_words, w1_scales, w2, gain, w3,
+    slope, thr, tint, shade0, wgs, gain2, w4_words, w4_scales, tone, out,
+):
+    nc = tc.nc
+    with ExitStack() as ctx:
+        keep = ctx.enter_context(tc.tile_pool(name="keep", bufs=1))
+        ring = ctx.enter_context(tc.tile_pool(name="ring", bufs=1))
+        psum = ctx.enter_context(tc.psum_pool(name="psum", bufs=8))
+
+        def held(shape, dtype, name):
+            return keep.tile(shape, dtype, name=name, align_bytes=64)
+
+        def staged():
+            return ring.tile([P, PACK * HALF], BF16, name="staged", tag="staged", bufs=6, align_bytes=64)
+
+        def bank():
+            return psum.tile([P, HALF], F32, name="bank", tag="bank")
+
+        offs_sb = held([P, S // 16], U16, "offs_sb")
+        pos1_sb = held([P, LOOKS // 16], U16, "pos1_sb")
+        pos2_sb = held([P, LOOKS // 16], U16, "pos2_sb")
+        tabs = held([P, T], U8, "tabs")
+        w1s_raw = held([P, 2, M], U8, "w1s_raw")
+        gs = [held([P, S], U8, "gs0"), held([P, S], U8, "gs1")]
+        w4s = held([P, 2, N], U8, "w4s")
+        nc.vector.memset(tabs[:].bitcast(I32), 0)
+        nc.vector.memset(w1s_raw[:].bitcast(I32), 0)
+        nc.vector.memset(gs[1][:].bitcast(I32), 0)
+        nc.vector.memset(w4s[:].bitcast(I32), 0)
+
+        nc.sync.dma_start(offs_sb[:], offs)
+        tabw = [held([P, T], U32, "tabw%d" % a) for a in range(2)]
+        w1w_raw = held([P, 2, 2 * M], U8, "w1w_raw")
+        nc.sync.dma_start(w1w_raw[:].bitcast(I32), w1_words.rearrange("a p c -> p a c").bitcast(I32))
+        for q in range(4):
+            nc.sync.dma_start(tabs[32 * q : 32 * q + 8, :].bitcast(I32), tab_scales[:, 4 * q : 4 * q + 4, :].bitcast(I32))
+        nc.sync.dma_start(tabw[0][:].bitcast(I32), tab_words[0].rearrange("p t i -> p (t i)").bitcast(I32))
+        for q in range(4):
+            nc.sync.dma_start(
+                w1s_raw[32 * q : 32 * q + 4, :, :].bitcast(I32),
+                w1_scales[:, 4 * q : 4 * q + 4, :].rearrange("a r c -> r a c").bitcast(I32),
+            )
+        nc.sync.dma_start(tabw[1][:].bitcast(I32), tab_words[1].rearrange("p t i -> p (t i)").bitcast(I32))
+        w2_raw = [held([P, PACK, M], F32, "w2_raw%d" % a) for a in range(2)]
+        for a in range(2):
+            nc.sync.dma_start(w2_raw[a][:], w2[KP * a : KP * (a + 1), :].rearrange("(p j) c -> p j c", j=PACK))
+        gain_sb = held([P, PACK], F32, "gain_sb")
+        nc.sync.dma_start(gain_sb[:], gain.rearrange("(p i) -> p i", i=PACK))
+        w3_raw = [held([P, PACK, KP], F32, "w3_raw%d" % a) for a in range(2)]
+        nc.sync.dma_start(w3_raw[0][:], w3[:, 0:KP].rearrange("(p j) c -> p j c", j=PACK))
+        nc.sync.dma_start(pos1_sb[:], pos1)
+        nc.sync.dma_start(pos2_sb[:], pos2)
+        rows = {}
+        for name, vec in (("shade0", shade0), ("slope", slope), ("thr", thr), ("gain2", gain2)):
+            rows[name] = held([P, 2 * PACK], F32, name + "_sb")
+            nc.sync.dma_start(
+                rows[name][:].rearrange("p (a i) -> p a i", i=PACK), vec.rearrange("(a p i) -> p a i", a=2, i=PACK)
+            )
+        wgs_sb = held([P, PACK, LOOKS], F32, "wgs_sb")
+        for q in range(4):
+            nc.sync.dma_start(wgs_sb[32 * q : 32 * q + 32, :, :], wgs.rearrange("(p i) j -> p i j", i=PACK))
+        tint_sb = [held([P, PACK, LOOKS], F32, "tint_sb%d" % a) for a in range(2)]
+        nc.sync.dma_start(tint_sb[0][:], tint[0:KP, :].rearrange("(p i) j -> p i j", i=PACK))
+        nc.sync.dma_start(w3_raw[1][:], w3[:, KP : 2 * KP].rearrange("(p j) c -> p j c", j=PACK))
+        nc.sync.dma_start(tint_sb[1][:], tint[KP : 2 * KP, :].rearrange("(p i) j -> p i j", i=PACK))
+        w4w = held([P, 2, N], U32, "w4w")
+        nc.sync.dma_start(w4w[:].bitcast(I32), w4_words.rearrange("a p c i -> p a (c i)").bitcast(I32))
+
+        for q in range(4):
+            nc.sync.dma_start(
+                w4s[32 * q : 32 * q + 4, :, :].bitcast(I32),
+                w4_scales[:, 4 * q : 4 * q + 4, :].rearrange("a r c -> r a c").bitcast(I32),
+            )
+        tone_sb = held([P, N // P], F32, "tone_sb")
+        with nc.allow_non_contiguous_dma(reason="one value a partition"):
+            nc.sync.dma_start(tone_sb[:], tone.rearrange("(c p) -> p c", p=P))
+
+        nc.vector.tensor_copy(gs[0][:], tabs[:].indirect(offs_sb[:]))
+        nc.scalar.dma_start(gs[1][0:112, :].bitcast(I32), gs[0][4:116, :].bitcast(I32))
+
+        gw = [[held([P, HALF], U32, "gw%d%d" % (a, hh)) for hh in range(2)] for a in range(2)]
+
+        def gather_words(a, hh):
+            nc.vector.tensor_copy(gw[a][hh][:], tabw[a][:].indirect(offs_sb[:, 32 * hh : 32 * (hh + 1)]))
+
+        gather_words(0, 0)
+        w1w = held([P, 2, 2 * M], U8, "w1w")
+        w1s = held([P, 2, M], U8, "w1s")
+        nc.vector.tensor_copy(
+            w1w[:].bitcast(U16).rearrange("p a (t q) -> p a t q", t=PACK),
+            w1w_raw[:].bitcast(U16).rearrange("p a (q t) -> p a t q", t=PACK),
+        )
+        nc.vector.tensor_copy(
+            w1s[:].rearrange("p a (t q) -> p a t q", t=PACK), w1s_raw[:].rearrange("p a (q t) -> p a t q", t=PACK)
+        )
+        gather_words(0, 1)
+        gather_words(1, 0)
+        gather_words(1, 1)
+
+        def deal_views(raw, dst, q0, q1):
+            return (
+                dst[:].rearrange("p (t q j) -> p q j t", t=PACK, j=PACK)[:, q0:q1],
+                raw[:].rearrange("p j (q t) -> p q j t", t=PACK)[:, q0:q1],
+            )
+
+        def quantise(src, name):
+            codes = held([P, HALF], U32, name + "c")
+            scales = held([P, HALF], U8, name + "s")
+            nc.vector.quantize_mx(out=codes[:].bitcast(FP8X4), scales=scales[:], in_=src[:])
+            return codes, scales
+
+        w2b = [staged(), staged()]
+        nc.scalar.copy(*deal_views(w2_raw[0], w2b[0], 0, P))
+        nc.vector.tensor_copy(*deal_views(w2_raw[1], w2b[1], 0, P))
+        w2q = [quantise(w2b[a], "w2q%d" % a) for a in range(2)]
+
+        e1 = {}
+        e1_banks = {(hh, i): bank() for hh in range(2) for i in range(PACK)}
+        for a in range(2):
+            for hh in range(2):
+                for i in range(PACK):
+                    nc.tensor.matmul_mx(
+                        out=e1_banks[hh, i][:],
+                        lhsT=w1w[:, a, 2 * P * i : 2 * P * (i + 1)].bitcast(FP4X4),
+                        lhsT_scale=w1s[:, a, P * i : P * (i + 1)],
+                        rhs=gw[a][hh][:].bitcast(FP8X4),
+                        rhs_scale=gs[a][:, HALF * hh : HALF * (hh + 1)],
+                        start=(a == 0), stop=(a == 1),
+                    )
+                    if a == 1:
+                        e1[hh, i] = held([P, HALF], F32, "e1_%d%d" % (hh, i))
+                        nc.scalar.copy(e1[hh, i][:], e1_banks[hh, i][:])
+
+        def interleave_views(plain, cols, dst):
+            return (
+                dst[:].rearrange("p (c i t) -> p c t i", i=PACK, t=PACK),
+                plain[:, :, cols].rearrange("p t (c i) -> p c t i", i=PACK),
+            )
+
+        eq = []
+        for hh in range(2):
+            plain = staged()
+            rows4 = plain[:].rearrange("p (t c) -> p t c", t=PACK)
+            for i in range(PACK):
+                acc = bank()
+                for a in range(2):
+                    nc.tensor.matmul_mx(
+                        out=acc[:],
+                        lhsT=w2q[a][0][:, P * i : P * (i + 1)].bitcast(FP8X4),
+                        lhsT_scale=w2q[a][1][:, P * i : P * (i + 1)],
+                        rhs=gw[a][hh][:].bitcast(FP8X4),
+                        rhs_scale=gs[a][:, HALF * hh : HALF * (hh + 1)],
+                        start=(a == 0), stop=(a == 1),
+                    )
+                nc.vector.tensor_tensor(e1[hh, i][:], acc[:], e1[hh, i][:], ALU.max)
+                if hh == 0:
+                    nc.scalar.activation(rows4[:, i, :], e1[hh, i][:], ACT.Copy, scale=gain_sb[:, i : i + 1])
+                else:
+                    nc.vector.tensor_scalar(rows4[:, i, :], e1[hh, i][:], gain_sb[:, i : i + 1], None, ALU.mult)
+            woven = staged()
+            nc.vector.tensor_copy(*interleave_views(rows4, slice(0, HALF), woven))
+            eq.append(quantise(woven, "eq%d" % hh))
+
+        w3q = []
+
+        def prepare_w3(a):
+            w3b = staged()
+            for q0 in range(0, P, 32):
+                nc.scalar.copy(*deal_views(w3_raw[a], w3b, q0, q0 + 32))
+            w3q.append(quantise(w3b, "w3q%d" % a))
+
+        prepare_w3(0)
+
+        pages = {}
+        yplain = [held([P, PACK, S], BF16, "yplain%d" % a) for a in range(2)]
+        outs = {}
+
+        def look_and_put(k):
+            a, t = divmod(k, PACK)
+            col = slice(k, k + 1)
+            h = ring.tile([P, S], F32, name="h", tag="h", bufs=3)
+            page = ring.tile([P, S], F32, name="page", tag="page", bufs=4)
+            accs = []
+            for hh in range(2):
+                acc = bank()
+                nc.tensor.matmul_mx(
+                    out=acc[:],
+                    lhsT=w3q[a][0][:, P * t : P * (t + 1)].bitcast(FP8X4),
+                    lhsT_scale=w3q[a][1][:, P * t : P * (t + 1)],
+                    rhs=eq[hh][0][:].bitcast(FP8X4),
+                    rhs_scale=eq[hh][1][:],
+                    start=True, stop=True,
+                )
+                nc.scalar.copy(h[:, HALF * hh : HALF * (hh + 1)], acc[:])
+                accs.append(acc)
+            if k == 0:
+                nc.vector.tensor_scalar(page[:], h[:], rows["shade0"][:, col], None, ALU.add)
+            else:
+                for hh in range(2):
+                    nc.scalar.activation(
+                        page[:, HALF * hh : HALF * (hh + 1)], accs[hh][:], ACT.Identity, bias=rows["shade0"][:, col]
+                    )
+            look = ring.tile([P, LOOKS], F32, name="look", tag="look", bufs=3)
+            nc.scalar.activation(
+                out=look[:], in_=h[:].indirect(pos1_sb[:]), func=ACT.Sigmoid,
+                bias=rows["thr"][:, col], scale=rows["slope"][:, col],
+            )
+            nc.vector.tensor_tensor(tint_sb[a][:, t, :], tint_sb[a][:, t, :], wgs_sb[:, t, :], ALU.mult)
+            nc.vector.tensor_tensor(page[:].indirect(pos2_sb[:]), look[:], tint_sb[a][:, t, :], ALU.mult)
+            pages[k] = page
+
+        def round_page(k):
+            a, t = divmod(k, PACK)
+            nc.scalar.activation(yplain[a][:, t, :], pages[k][:], ACT.Copy, scale=rows["gain2"][:, k : k + 1])
+
+        def multiply(a, codes, scales, j0, width):
+            hh, lo = divmod(j0, HALF)
+            for c in range(N // P):
+                nc.tensor.matmul_mx(
+                    out=outs[hh, c][:, lo : lo + width],
+                    lhsT=w4w[:, a, P * c : P * (c + 1)].bitcast(FP8X4),
+                    lhsT_scale=w4s[:, a, P * c : P * (c + 1)],
+                    rhs=codes.bitcast(FP8X4),
+                    rhs_scale=scales,
+                    start=(a == 0), stop=(a == 1),
+                )
+
+        def first_block():
+            for hh in range(2):
+                woven = staged()
+                nc.vector.tensor_copy(*interleave_views(yplain[0], slice(HALF * hh, HALF * (hh + 1)), woven))
+                codes, scales = quantise(woven, "yq0%d" % hh)
+                for c in range(N // P):
+                    outs[hh, c] = bank()
+                multiply(0, codes[:], scales[:], HALF * hh, HALF)
+
+        def last_block():
+            k = H // P - 1
+            gcol = rows["gain2"][:, k : k + 1]
+            nc.vector.tensor_scalar(yplain[1][:, PACK - 1, 0:HALF], pages[k][:, 0:HALF], gcol, None, ALU.mult)
+            nc.scalar.activation(yplain[1][:, PACK - 1, HALF:S], pages[k][:, HALF:S], ACT.Copy, scale=gcol)
+            woven = [staged(), staged()]
+            nc.vector.tensor_copy(*interleave_views(yplain[1], slice(0, HALF), woven[0]))
+            out_s, in_s = interleave_views(yplain[1], slice(HALF, S), woven[1])
+            nc.scalar.copy(out_s[:, 0:64], in_s[:, 0:64])
+            for hh in range(2):
+                if hh == 1:
+                    nc.vector.tensor_copy(out_s[:, 64:128], in_s[:, 64:128])
+                codes, scales = quantise(woven[hh], "yq1%d" % hh)
+                multiply(1, codes[:], scales[:], HALF * hh, HALF)
+                for c in range(N // P):
+                    res = ring.tile([P, HALF], F32, name="res", tag="res", bufs=8)
+                    if hh == 0 or c % 2 == 0:
+                        nc.scalar.activation(res[:], outs[hh, c][:], ACT.Copy, scale=tone_sb[:, c : c + 1])
+                    else:
+                        nc.vector.tensor_scalar(res[:], outs[hh, c][:], tone_sb[:, c : c + 1], None, ALU.mult)
+                    nc.sync.dma_start(out[P * c : P * (c + 1), HALF * hh : HALF * (hh + 1)], res[:])
+
+        tiles = H // P
+        for k in range(tiles):
+            look_and_put(k)
+            if k == 1:
+                prepare_w3(1)
+            if k >= 1:
+                round_page(k - 1)
+        first_block()
+        last_block()

@@ -36,7 +36,7 @@ def tile_list_indigo_shade_readout_kernel(
             return keep.tile(shape, dtype, name=name, align_bytes=64)
 
         def staged():
-            return ring.tile([P, PACK * HALF], BF16, name="staged", tag="staged", bufs=6, align_bytes=64)
+            return ring.tile([P, PACK * HALF], BF16, name="staged", tag="staged", bufs=8, align_bytes=64)
 
         def bank():
             return psum.tile([P, HALF], F32, name="bank", tag="bank")
@@ -53,50 +53,75 @@ def tile_list_indigo_shade_readout_kernel(
         nc.vector.memset(gs[1][:].bitcast(I32), 0)
         nc.vector.memset(w4s[:].bitcast(I32), 0)
 
-        nc.sync.dma_start(offs_sb[:], offs)
+        warm_in = held([P, 1], F32, "warm_in")
+        warm_out = held([P, 1], F32, "warm_out")
+        nc.gpsimd.memset(warm_in[:], 0.0)
+        nc.scalar.activation(warm_out[:], warm_in[:], ACT.Sigmoid)
+
         tabw = [held([P, T], U32, "tabw%d" % a) for a in range(2)]
         w1w_raw = held([P, 2, 2 * M], U8, "w1w_raw")
-        nc.sync.dma_start(w1w_raw[:].bitcast(I32), w1_words.rearrange("a p c -> p a c").bitcast(I32))
-        for q in range(4):
-            nc.sync.dma_start(tabs[32 * q : 32 * q + 8, :].bitcast(I32), tab_scales[:, 4 * q : 4 * q + 4, :].bitcast(I32))
-        nc.sync.dma_start(tabw[0][:].bitcast(I32), tab_words[0].rearrange("p t i -> p (t i)").bitcast(I32))
-        for q in range(4):
-            nc.sync.dma_start(
-                w1s_raw[32 * q : 32 * q + 4, :, :].bitcast(I32),
-                w1_scales[:, 4 * q : 4 * q + 4, :].rearrange("a r c -> r a c").bitcast(I32),
-            )
-        nc.sync.dma_start(tabw[1][:].bitcast(I32), tab_words[1].rearrange("p t i -> p (t i)").bitcast(I32))
         w2_raw = [held([P, PACK, M], F32, "w2_raw%d" % a) for a in range(2)]
-        for a in range(2):
-            nc.sync.dma_start(w2_raw[a][:], w2[KP * a : KP * (a + 1), :].rearrange("(p j) c -> p j c", j=PACK))
-        gain_sb = held([P, PACK], F32, "gain_sb")
-        nc.sync.dma_start(gain_sb[:], gain.rearrange("(p i) -> p i", i=PACK))
         w3_raw = [held([P, PACK, KP], F32, "w3_raw%d" % a) for a in range(2)]
-        nc.sync.dma_start(w3_raw[0][:], w3[:, 0:KP].rearrange("(p j) c -> p j c", j=PACK))
-        nc.sync.dma_start(pos1_sb[:], pos1)
-        nc.sync.dma_start(pos2_sb[:], pos2)
+        gain_sb = held([P, PACK], F32, "gain_sb")
+        wgs_sb = held([P, PACK, LOOKS], F32, "wgs_sb")
+        slots = held([P, (H // P + 1) * LOOKS], F32, "slots")
+        w4w = held([P, 2, N], U32, "w4w")
+        tone_sb = held([P, N // P], F32, "tone_sb")
         rows = {}
-        for name, vec in (("shade0", shade0), ("slope", slope), ("thr", thr), ("gain2", gain2)):
+
+        def slot(k, n=1):
+            return slots[:, LOOKS * k : LOOKS * (k + n)]
+
+        def load_tab(a):
+            nc.sync.dma_start(tabw[a][:].bitcast(I32), tab_words[a].rearrange("p t i -> p (t i)").bitcast(I32))
+
+        def load_w2(a):
+            nc.sync.dma_start(w2_raw[a][:], w2[KP * a : KP * (a + 1), :].rearrange("(p j) c -> p j c", j=PACK))
+
+        def load_w3(a):
+            nc.sync.dma_start(w3_raw[a][:], w3[:, KP * a : KP * (a + 1)].rearrange("(p j) c -> p j c", j=PACK))
+
+        def load_tint(a):
+            nc.sync.dma_start(slot(PACK * a, PACK), tint[KP * a : KP * (a + 1), :].rearrange("(p i) j -> p (i j)", i=PACK))
+
+        def load_row_values(name, vec):
             rows[name] = held([P, 2 * PACK], F32, name + "_sb")
             nc.sync.dma_start(
                 rows[name][:].rearrange("p (a i) -> p a i", i=PACK), vec.rearrange("(a p i) -> p a i", a=2, i=PACK)
             )
-        wgs_sb = held([P, PACK, LOOKS], F32, "wgs_sb")
+
+        def load_scale_rows(dst, src, q):
+            nc.sync.dma_start(
+                dst[32 * q : 32 * q + 4, :, :].bitcast(I32),
+                src[:, 4 * q : 4 * q + 4, :].rearrange("a r c -> r a c").bitcast(I32),
+            )
+
+        nc.sync.dma_start(offs_sb[:], offs)
+        nc.sync.dma_start(w1w_raw[:].bitcast(I32), w1_words.rearrange("a p c -> p a c").bitcast(I32))
+        for q in range(4):
+            nc.sync.dma_start(tabs[32 * q : 32 * q + 8, :].bitcast(I32), tab_scales[:, 4 * q : 4 * q + 4, :].bitcast(I32))
+        load_tab(0)
+        for q in range(4):
+            load_scale_rows(w1s_raw, w1_scales, q)
+        load_w2(0)
+        load_tab(1)
+        load_w2(1)
+        nc.sync.dma_start(gain_sb[:], gain.rearrange("(p i) -> p i", i=PACK))
+        load_w3(0)
+        nc.sync.dma_start(pos1_sb[:], pos1)
+        load_row_values("slope", slope)
+        load_w3(1)
+        load_row_values("thr", thr)
+        load_row_values("shade0", shade0)
+        load_tint(0)
         for q in range(4):
             nc.sync.dma_start(wgs_sb[32 * q : 32 * q + 32, :, :], wgs.rearrange("(p i) j -> p i j", i=PACK))
-        tint_sb = [held([P, PACK, LOOKS], F32, "tint_sb%d" % a) for a in range(2)]
-        nc.sync.dma_start(tint_sb[0][:], tint[0:KP, :].rearrange("(p i) j -> p i j", i=PACK))
-        nc.sync.dma_start(w3_raw[1][:], w3[:, KP : 2 * KP].rearrange("(p j) c -> p j c", j=PACK))
-        nc.sync.dma_start(tint_sb[1][:], tint[KP : 2 * KP, :].rearrange("(p i) j -> p i j", i=PACK))
-        w4w = held([P, 2, N], U32, "w4w")
+        nc.sync.dma_start(pos2_sb[:], pos2)
+        load_row_values("gain2", gain2)
+        load_tint(1)
         nc.sync.dma_start(w4w[:].bitcast(I32), w4_words.rearrange("a p c i -> p a (c i)").bitcast(I32))
-
         for q in range(4):
-            nc.sync.dma_start(
-                w4s[32 * q : 32 * q + 4, :, :].bitcast(I32),
-                w4_scales[:, 4 * q : 4 * q + 4, :].rearrange("a r c -> r a c").bitcast(I32),
-            )
-        tone_sb = held([P, N // P], F32, "tone_sb")
+            load_scale_rows(w4s, w4_scales, q)
         with nc.allow_non_contiguous_dma(reason="one value a partition"):
             nc.sync.dma_start(tone_sb[:], tone.rearrange("(c p) -> p c", p=P))
 
@@ -136,8 +161,10 @@ def tile_list_indigo_shade_readout_kernel(
 
         w2b = [staged(), staged()]
         nc.scalar.copy(*deal_views(w2_raw[0], w2b[0], 0, P))
-        nc.vector.tensor_copy(*deal_views(w2_raw[1], w2b[1], 0, P))
-        w2q = [quantise(w2b[a], "w2q%d" % a) for a in range(2)]
+        nc.scalar.copy(*deal_views(w2_raw[1], w2b[1], 0, P // 2))
+        w2q = [quantise(w2b[0], "w2q0")]
+        nc.vector.tensor_copy(*deal_views(w2_raw[1], w2b[1], P // 2, P))
+        w2q.append(quantise(w2b[1], "w2q1"))
 
         e1 = {}
         e1_banks = {(hh, i): bank() for hh in range(2) for i in range(PACK)}
@@ -162,10 +189,11 @@ def tile_list_indigo_shade_readout_kernel(
                 plain[:, :, cols].rearrange("p t (c i) -> p c t i", i=PACK),
             )
 
-        eq = []
+        eplain = []
         for hh in range(2):
             plain = staged()
             rows4 = plain[:].rearrange("p (t c) -> p t c", t=PACK)
+            eplain.append(rows4)
             for i in range(PACK):
                 acc = bank()
                 for a in range(2):
@@ -178,13 +206,7 @@ def tile_list_indigo_shade_readout_kernel(
                         start=(a == 0), stop=(a == 1),
                     )
                 nc.vector.tensor_tensor(e1[hh, i][:], acc[:], e1[hh, i][:], ALU.max)
-                if hh == 0:
-                    nc.scalar.activation(rows4[:, i, :], e1[hh, i][:], ACT.Copy, scale=gain_sb[:, i : i + 1])
-                else:
-                    nc.vector.tensor_scalar(rows4[:, i, :], e1[hh, i][:], gain_sb[:, i : i + 1], None, ALU.mult)
-            woven = staged()
-            nc.vector.tensor_copy(*interleave_views(rows4, slice(0, HALF), woven))
-            eq.append(quantise(woven, "eq%d" % hh))
+                nc.gpsimd.tensor_scalar(rows4[:, i, :], e1[hh, i][:], gain_sb[:, i : i + 1], 0.0, ALU.mult, ALU.add)
 
         w3q = []
 
@@ -194,10 +216,15 @@ def tile_list_indigo_shade_readout_kernel(
                 nc.scalar.copy(*deal_views(w3_raw[a], w3b, q0, q0 + 32))
             w3q.append(quantise(w3b, "w3q%d" % a))
 
+        woven = [staged(), staged()]
+        nc.scalar.copy(*interleave_views(eplain[0], slice(0, HALF), woven[0]))
+        eq = [quantise(woven[0], "eq0")]
+        nc.vector.tensor_copy(*interleave_views(eplain[1], slice(0, HALF), woven[1]))
+        eq.append(quantise(woven[1], "eq1"))
         prepare_w3(0)
 
         pages = {}
-        yplain = [held([P, PACK, S], BF16, "yplain%d" % a) for a in range(2)]
+        yplain = [slot(PACK * a + 1, PACK).bitcast(BF16).rearrange("p (t c) -> p t c", t=PACK) for a in range(2)]
         outs = {}
 
         def look_and_put(k):
@@ -226,17 +253,27 @@ def tile_list_indigo_shade_readout_kernel(
                         page[:, HALF * hh : HALF * (hh + 1)], accs[hh][:], ACT.Identity, bias=rows["shade0"][:, col]
                     )
             look = ring.tile([P, LOOKS], F32, name="look", tag="look", bufs=3)
-            nc.scalar.activation(
-                out=look[:], in_=h[:].indirect(pos1_sb[:]), func=ACT.Sigmoid,
-                bias=rows["thr"][:, col], scale=rows["slope"][:, col],
-            )
-            nc.vector.tensor_tensor(tint_sb[a][:, t, :], tint_sb[a][:, t, :], wgs_sb[:, t, :], ALU.mult)
-            nc.vector.tensor_tensor(page[:].indirect(pos2_sb[:]), look[:], tint_sb[a][:, t, :], ALU.mult)
+            parts = 2 if k == 0 else 1
+            width = LOOKS // parts
+            for part in range(parts):
+                cols = slice(width * part, width * (part + 1))
+                entries = slice(width * part // 16, width * (part + 1) // 16)
+                nc.scalar.activation(
+                    out=look[:, cols], in_=h[:].indirect(pos1_sb[:, entries]), func=ACT.Sigmoid,
+                    bias=rows["thr"][:, col], scale=rows["slope"][:, col],
+                )
+                if k == 0:
+                    nc.vector.tensor_tensor(look[:, cols], look[:, cols], slot(k)[:, cols], ALU.mult)
+                else:
+                    nc.gpsimd.tensor_tensor(look[:, cols], look[:, cols], slot(k)[:, cols], ALU.mult)
+                nc.vector.tensor_copy(page[:].indirect(pos2_sb[:, entries]), look[:, cols])
             pages[k] = page
 
         def round_page(k):
             a, t = divmod(k, PACK)
-            nc.scalar.activation(yplain[a][:, t, :], pages[k][:], ACT.Copy, scale=rows["gain2"][:, k : k + 1])
+            nc.gpsimd.tensor_scalar(
+                slot(k + 1).bitcast(BF16), pages[k][:], rows["gain2"][:, k : k + 1], 0.0, ALU.mult, ALU.add
+            )
 
         def multiply(a, codes, scales, j0, width):
             hh, lo = divmod(j0, HALF)
@@ -250,11 +287,16 @@ def tile_list_indigo_shade_readout_kernel(
                     start=(a == 0), stop=(a == 1),
                 )
 
+        yq0 = []
+
+        def weave_first(hh):
+            woven = staged()
+            nc.scalar.copy(*interleave_views(yplain[0], slice(HALF * hh, HALF * (hh + 1)), woven))
+            yq0.append(quantise(woven, "yq0%d" % hh))
+
         def first_block():
             for hh in range(2):
-                woven = staged()
-                nc.vector.tensor_copy(*interleave_views(yplain[0], slice(HALF * hh, HALF * (hh + 1)), woven))
-                codes, scales = quantise(woven, "yq0%d" % hh)
+                codes, scales = yq0[hh]
                 for c in range(N // P):
                     outs[hh, c] = bank()
                 multiply(0, codes[:], scales[:], HALF * hh, HALF)
@@ -282,11 +324,17 @@ def tile_list_indigo_shade_readout_kernel(
                     nc.sync.dma_start(out[P * c : P * (c + 1), HALF * hh : HALF * (hh + 1)], res[:])
 
         tiles = H // P
+        for t in range(PACK):
+            nc.vector.tensor_tensor(slot(t), slot(t), wgs_sb[:, t, :], ALU.mult)
+        for t in range(PACK):
+            nc.gpsimd.tensor_tensor(slot(PACK + t), slot(PACK + t), wgs_sb[:, t, :], ALU.mult)
         for k in range(tiles):
             look_and_put(k)
-            if k == 1:
+            if k == 0:
                 prepare_w3(1)
             if k >= 1:
                 round_page(k - 1)
+        weave_first(0)
+        weave_first(1)
         first_block()
         last_block()

@@ -20,6 +20,11 @@ P = 128
 PACK = 4
 KP = P * PACK
 HALF = 512
+QUAD = 32
+QUADS = P // QUAD
+PER_COLUMN = 16
+ROW_TILES = H // P
+ROUNDED_ON_VECTOR = (1, 3)
 
 
 def tile_list_indigo_shade_readout_kernel(
@@ -38,42 +43,43 @@ def tile_list_indigo_shade_readout_kernel(
         def staged():
             return ring.tile([P, PACK * HALF], BF16, name="staged", tag="staged", bufs=8, align_bytes=64)
 
+        def row_tile():
+            return ring.tile([P, S], F32, name="row_tile", tag="row_tile", bufs=6)
+
         def bank():
             return psum.tile([P, HALF], F32, name="bank", tag="bank")
 
-        offs_sb = held([P, S // 16], U16, "offs_sb")
-        pos1_sb = held([P, LOOKS // 16], U16, "pos1_sb")
-        pos2_sb = held([P, LOOKS // 16], U16, "pos2_sb")
-        tabs = held([P, T], U8, "tabs")
-        w1s_raw = held([P, 2, M], U8, "w1s_raw")
-        gs = [held([P, S], U8, "gs0"), held([P, S], U8, "gs1")]
-        w4s = held([P, 2, N], U8, "w4s")
-        nc.vector.memset(tabs[:].bitcast(I32), 0)
-        nc.vector.memset(w1s_raw[:].bitcast(I32), 0)
-        nc.vector.memset(gs[1][:].bitcast(I32), 0)
-        nc.vector.memset(w4s[:].bitcast(I32), 0)
+        def half(hh):
+            return slice(HALF * hh, HALF * (hh + 1))
 
-        warm_in = held([P, 1], F32, "warm_in")
-        warm_out = held([P, 1], F32, "warm_out")
-        nc.gpsimd.memset(warm_in[:], 0.0)
-        nc.scalar.activation(warm_out[:], warm_in[:], ACT.Sigmoid)
+        offs_sb = held([P, S // PER_COLUMN], U16, "offs_sb")
+        pos1_sb = held([P, LOOKS // PER_COLUMN], U16, "pos1_sb")
+        pos2_sb = held([P, LOOKS // PER_COLUMN], U16, "pos2_sb")
+        tab_scale_sb = held([P, T], U8, "tab_scale_sb")
+        w1_scale_raw = held([P, 2, M], U8, "w1_scale_raw")
+        picked_scales = [held([P, S], U8, "picked_scales0"), held([P, S], U8, "picked_scales1")]
+        w4_scale_sb = held([P, 2, N], U8, "w4_scale_sb")
+        nc.vector.memset(tab_scale_sb[:].bitcast(I32), 0)
+        nc.vector.memset(w1_scale_raw[:].bitcast(I32), 0)
+        nc.vector.memset(picked_scales[1][:].bitcast(I32), 0)
+        nc.vector.memset(w4_scale_sb[:].bitcast(I32), 0)
 
-        tabw = [held([P, T], U32, "tabw%d" % a) for a in range(2)]
-        w1w_raw = held([P, 2, 2 * M], U8, "w1w_raw")
+        tab_word_sb = [held([P, T], U32, "tab_word_sb%d" % a) for a in range(2)]
+        w1_word_raw = held([P, 2, 2 * M], U8, "w1_word_raw")
         w2_raw = [held([P, PACK, M], F32, "w2_raw%d" % a) for a in range(2)]
         w3_raw = [held([P, PACK, KP], F32, "w3_raw%d" % a) for a in range(2)]
         gain_sb = held([P, PACK], F32, "gain_sb")
         wgs_sb = held([P, PACK, LOOKS], F32, "wgs_sb")
-        slots = held([P, (H // P + 1) * LOOKS], F32, "slots")
-        w4w = held([P, 2, N], U32, "w4w")
+        tint_sb = held([P, ROW_TILES * LOOKS], F32, "tint_sb")
+        w4_word_sb = held([P, 2, N], U32, "w4_word_sb")
         tone_sb = held([P, N // P], F32, "tone_sb")
-        rows = {}
+        row_values = {}
 
-        def slot(k, n=1):
-            return slots[:, LOOKS * k : LOOKS * (k + n)]
+        def tint_of(k, n=1):
+            return tint_sb[:, LOOKS * k : LOOKS * (k + n)]
 
         def load_tab(a):
-            nc.sync.dma_start(tabw[a][:].bitcast(I32), tab_words[a].rearrange("p t i -> p (t i)").bitcast(I32))
+            nc.sync.dma_start(tab_word_sb[a][:].bitcast(I32), tab_words[a].rearrange("p t i -> p (t i)").bitcast(I32))
 
         def load_w2(a):
             nc.sync.dma_start(w2_raw[a][:], w2[KP * a : KP * (a + 1), :].rearrange("(p j) c -> p j c", j=PACK))
@@ -81,28 +87,32 @@ def tile_list_indigo_shade_readout_kernel(
         def load_w3(a):
             nc.sync.dma_start(w3_raw[a][:], w3[:, KP * a : KP * (a + 1)].rearrange("(p j) c -> p j c", j=PACK))
 
-        def load_tint(a):
-            nc.sync.dma_start(slot(PACK * a, PACK), tint[KP * a : KP * (a + 1), :].rearrange("(p i) j -> p (i j)", i=PACK))
+        def load_tint(k, n):
+            a, t = divmod(k, PACK)
+            four_rows = tint[KP * a : KP * (a + 1), :].rearrange("(p i) j -> p (i j)", i=PACK)
+            nc.sync.dma_start(tint_of(k, n), four_rows[:, LOOKS * t : LOOKS * (t + n)])
 
         def load_row_values(name, vec):
-            rows[name] = held([P, 2 * PACK], F32, name + "_sb")
+            row_values[name] = held([P, ROW_TILES], F32, name + "_sb")
             nc.sync.dma_start(
-                rows[name][:].rearrange("p (a i) -> p a i", i=PACK), vec.rearrange("(a p i) -> p a i", a=2, i=PACK)
+                row_values[name][:].rearrange("p (a i) -> p a i", i=PACK), vec.rearrange("(a p i) -> p a i", a=2, i=PACK)
             )
 
         def load_scale_rows(dst, src, q):
             nc.sync.dma_start(
-                dst[32 * q : 32 * q + 4, :, :].bitcast(I32),
+                dst[QUAD * q : QUAD * q + 4, :, :].bitcast(I32),
                 src[:, 4 * q : 4 * q + 4, :].rearrange("a r c -> r a c").bitcast(I32),
             )
 
         nc.sync.dma_start(offs_sb[:], offs)
-        nc.sync.dma_start(w1w_raw[:].bitcast(I32), w1_words.rearrange("a p c -> p a c").bitcast(I32))
-        for q in range(4):
-            nc.sync.dma_start(tabs[32 * q : 32 * q + 8, :].bitcast(I32), tab_scales[:, 4 * q : 4 * q + 4, :].bitcast(I32))
+        nc.sync.dma_start(w1_word_raw[:].bitcast(I32), w1_words.rearrange("a p c -> p a c").bitcast(I32))
+        for q in range(QUADS):
+            nc.sync.dma_start(
+                tab_scale_sb[QUAD * q : QUAD * q + 8, :].bitcast(I32), tab_scales[:, 4 * q : 4 * q + 4, :].bitcast(I32)
+            )
         load_tab(0)
-        for q in range(4):
-            load_scale_rows(w1s_raw, w1_scales, q)
+        for q in range(QUADS):
+            load_scale_rows(w1_scale_raw, w1_scales, q)
         load_w2(0)
         load_tab(1)
         load_w2(1)
@@ -113,35 +123,39 @@ def tile_list_indigo_shade_readout_kernel(
         load_w3(1)
         load_row_values("thr", thr)
         load_row_values("shade0", shade0)
-        load_tint(0)
-        for q in range(4):
-            nc.sync.dma_start(wgs_sb[32 * q : 32 * q + 32, :, :], wgs.rearrange("(p i) j -> p i j", i=PACK))
+        for q in range(QUADS):
+            nc.sync.dma_start(wgs_sb[QUAD * q : QUAD * (q + 1), :, :], wgs.rearrange("(p i) j -> p i j", i=PACK))
+        load_tint(0, 2)
         nc.sync.dma_start(pos2_sb[:], pos2)
+        load_tint(2, 2)
         load_row_values("gain2", gain2)
-        load_tint(1)
-        nc.sync.dma_start(w4w[:].bitcast(I32), w4_words.rearrange("a p c i -> p a (c i)").bitcast(I32))
-        for q in range(4):
-            load_scale_rows(w4s, w4_scales, q)
+        load_tint(PACK, PACK)
+        nc.sync.dma_start(w4_word_sb[:].bitcast(I32), w4_words.rearrange("a p c i -> p a (c i)").bitcast(I32))
+        for q in range(QUADS):
+            load_scale_rows(w4_scale_sb, w4_scales, q)
         with nc.allow_non_contiguous_dma(reason="one value a partition"):
             nc.sync.dma_start(tone_sb[:], tone.rearrange("(c p) -> p c", p=P))
 
-        nc.vector.tensor_copy(gs[0][:], tabs[:].indirect(offs_sb[:]))
-        nc.scalar.dma_start(gs[1][0:112, :].bitcast(I32), gs[0][4:116, :].bitcast(I32))
+        nc.vector.tensor_copy(picked_scales[0][:], tab_scale_sb[:].indirect(offs_sb[:]))
+        span = QUAD * (QUADS - 1) + 4
+        nc.scalar.dma_start(picked_scales[1][0:span, :].bitcast(I32), picked_scales[0][4 : 4 + span, :].bitcast(I32))
 
-        gw = [[held([P, HALF], U32, "gw%d%d" % (a, hh)) for hh in range(2)] for a in range(2)]
+        picked_words = [[held([P, HALF], U32, "picked_words%d%d" % (a, hh)) for hh in range(2)] for a in range(2)]
 
         def gather_words(a, hh):
-            nc.vector.tensor_copy(gw[a][hh][:], tabw[a][:].indirect(offs_sb[:, 32 * hh : 32 * (hh + 1)]))
+            entries = slice(HALF // PER_COLUMN * hh, HALF // PER_COLUMN * (hh + 1))
+            nc.vector.tensor_copy(picked_words[a][hh][:], tab_word_sb[a][:].indirect(offs_sb[:, entries]))
 
         gather_words(0, 0)
-        w1w = held([P, 2, 2 * M], U8, "w1w")
-        w1s = held([P, 2, M], U8, "w1s")
+        w1_word_sb = held([P, 2, 2 * M], U8, "w1_word_sb")
+        w1_scale_sb = held([P, 2, M], U8, "w1_scale_sb")
         nc.vector.tensor_copy(
-            w1w[:].bitcast(U16).rearrange("p a (t q) -> p a t q", t=PACK),
-            w1w_raw[:].bitcast(U16).rearrange("p a (q t) -> p a t q", t=PACK),
+            w1_word_sb[:].bitcast(U16).rearrange("p a (t q) -> p a t q", t=PACK),
+            w1_word_raw[:].bitcast(U16).rearrange("p a (q t) -> p a t q", t=PACK),
         )
         nc.vector.tensor_copy(
-            w1s[:].rearrange("p a (t q) -> p a t q", t=PACK), w1s_raw[:].rearrange("p a (q t) -> p a t q", t=PACK)
+            w1_scale_sb[:].rearrange("p a (t q) -> p a t q", t=PACK),
+            w1_scale_raw[:].rearrange("p a (q t) -> p a t q", t=PACK),
         )
         gather_words(0, 1)
         gather_words(1, 0)
@@ -154,187 +168,184 @@ def tile_list_indigo_shade_readout_kernel(
             )
 
         def quantise(src, name):
-            codes = held([P, HALF], U32, name + "c")
-            scales = held([P, HALF], U8, name + "s")
+            codes = held([P, HALF], U32, name + "_codes")
+            scales = held([P, HALF], U8, name + "_scales")
             nc.vector.quantize_mx(out=codes[:].bitcast(FP8X4), scales=scales[:], in_=src[:])
             return codes, scales
 
-        w2b = [staged(), staged()]
-        nc.scalar.copy(*deal_views(w2_raw[0], w2b[0], 0, P))
-        nc.scalar.copy(*deal_views(w2_raw[1], w2b[1], 0, P // 2))
-        w2q = [quantise(w2b[0], "w2q0")]
-        nc.vector.tensor_copy(*deal_views(w2_raw[1], w2b[1], P // 2, P))
-        w2q.append(quantise(w2b[1], "w2q1"))
+        w2_bf = [staged(), staged()]
+        nc.vector.tensor_copy(*deal_views(w2_raw[0], w2_bf[0], 0, P))
+        nc.scalar.copy(*deal_views(w2_raw[1], w2_bf[1], 0, P // 2))
+        w2_mx = [quantise(w2_bf[0], "w2_mx0")]
+        nc.vector.tensor_copy(*deal_views(w2_raw[1], w2_bf[1], P // 2, P))
+        w2_mx.append(quantise(w2_bf[1], "w2_mx1"))
 
-        e1 = {}
-        e1_banks = {(hh, i): bank() for hh in range(2) for i in range(PACK)}
+        joined = {}
+        w1_banks = {(hh, i): bank() for hh in range(2) for i in range(PACK)}
         for a in range(2):
             for hh in range(2):
                 for i in range(PACK):
                     nc.tensor.matmul_mx(
-                        out=e1_banks[hh, i][:],
-                        lhsT=w1w[:, a, 2 * P * i : 2 * P * (i + 1)].bitcast(FP4X4),
-                        lhsT_scale=w1s[:, a, P * i : P * (i + 1)],
-                        rhs=gw[a][hh][:].bitcast(FP8X4),
-                        rhs_scale=gs[a][:, HALF * hh : HALF * (hh + 1)],
+                        out=w1_banks[hh, i][:],
+                        lhsT=w1_word_sb[:, a, 2 * P * i : 2 * P * (i + 1)].bitcast(FP4X4),
+                        lhsT_scale=w1_scale_sb[:, a, P * i : P * (i + 1)],
+                        rhs=picked_words[a][hh][:].bitcast(FP8X4),
+                        rhs_scale=picked_scales[a][:, half(hh)],
                         start=(a == 0), stop=(a == 1),
                     )
                     if a == 1:
-                        e1[hh, i] = held([P, HALF], F32, "e1_%d%d" % (hh, i))
-                        nc.scalar.copy(e1[hh, i][:], e1_banks[hh, i][:])
+                        joined[hh, i] = held([P, HALF], F32, "joined%d%d" % (hh, i))
+                        nc.scalar.copy(joined[hh, i][:], w1_banks[hh, i][:])
 
-        def interleave_views(plain, cols, dst):
+        def weave_views(plain, cols, dst):
             return (
                 dst[:].rearrange("p (c i t) -> p c t i", i=PACK, t=PACK),
                 plain[:, :, cols].rearrange("p t (c i) -> p c t i", i=PACK),
             )
 
-        eplain = []
+        e_plain = []
         for hh in range(2):
-            plain = staged()
-            rows4 = plain[:].rearrange("p (t c) -> p t c", t=PACK)
-            eplain.append(rows4)
+            e_plain.append(staged()[:].rearrange("p (t c) -> p t c", t=PACK))
             for i in range(PACK):
                 acc = bank()
                 for a in range(2):
                     nc.tensor.matmul_mx(
                         out=acc[:],
-                        lhsT=w2q[a][0][:, P * i : P * (i + 1)].bitcast(FP8X4),
-                        lhsT_scale=w2q[a][1][:, P * i : P * (i + 1)],
-                        rhs=gw[a][hh][:].bitcast(FP8X4),
-                        rhs_scale=gs[a][:, HALF * hh : HALF * (hh + 1)],
+                        lhsT=w2_mx[a][0][:, P * i : P * (i + 1)].bitcast(FP8X4),
+                        lhsT_scale=w2_mx[a][1][:, P * i : P * (i + 1)],
+                        rhs=picked_words[a][hh][:].bitcast(FP8X4),
+                        rhs_scale=picked_scales[a][:, half(hh)],
                         start=(a == 0), stop=(a == 1),
                     )
-                nc.vector.tensor_tensor(e1[hh, i][:], acc[:], e1[hh, i][:], ALU.max)
-                nc.gpsimd.tensor_scalar(rows4[:, i, :], e1[hh, i][:], gain_sb[:, i : i + 1], 0.0, ALU.mult, ALU.add)
+                nc.vector.tensor_tensor(joined[hh, i][:], acc[:], joined[hh, i][:], ALU.max)
+                nc.gpsimd.tensor_scalar(
+                    e_plain[hh][:, i, :], joined[hh, i][:], gain_sb[:, i : i + 1], 0.0, ALU.mult, ALU.add
+                )
 
-        w3q = []
+        e_woven = [staged(), staged()]
+        nc.scalar.copy(*weave_views(e_plain[0], half(0), e_woven[0]))
+        e_mx = [quantise(e_woven[0], "e_mx0")]
+        nc.vector.tensor_copy(*weave_views(e_plain[1], half(0), e_woven[1]))
+        e_mx.append(quantise(e_woven[1], "e_mx1"))
 
-        def prepare_w3(a):
-            w3b = staged()
-            for q0 in range(0, P, 32):
-                nc.scalar.copy(*deal_views(w3_raw[a], w3b, q0, q0 + 32))
-            w3q.append(quantise(w3b, "w3q%d" % a))
+        w3_bf = staged()
+        for q0 in range(0, P, P // 4):
+            nc.scalar.copy(*deal_views(w3_raw[0], w3_bf, q0, q0 + P // 4))
+        w3_mx = [quantise(w3_bf, "w3_mx0")]
 
-        woven = [staged(), staged()]
-        nc.scalar.copy(*interleave_views(eplain[0], slice(0, HALF), woven[0]))
-        eq = [quantise(woven[0], "eq0")]
-        nc.vector.tensor_copy(*interleave_views(eplain[1], slice(0, HALF), woven[1]))
-        eq.append(quantise(woven[1], "eq1"))
-        prepare_w3(0)
+        def quantise_rest_of_w3():
+            rest_bf = staged()
+            nc.vector.tensor_copy(*deal_views(w3_raw[1], rest_bf, 0, P))
+            w3_mx.append(quantise(rest_bf, "w3_mx1"))
 
+        h_tiles = {}
         pages = {}
-        yplain = [slot(PACK * a + 1, PACK).bitcast(BF16).rearrange("p (t c) -> p t c", t=PACK) for a in range(2)]
-        outs = {}
+        y_plain = [held([P, PACK, S], BF16, "y_plain%d" % a) for a in range(2)]
 
         def look_and_put(k):
             a, t = divmod(k, PACK)
             col = slice(k, k + 1)
-            h = ring.tile([P, S], F32, name="h", tag="h", bufs=3)
-            page = ring.tile([P, S], F32, name="page", tag="page", bufs=4)
+            h = row_tile()
+            h_tiles[k] = h
+            page = row_tile() if k == 0 else h_tiles[k - 1]
             accs = []
             for hh in range(2):
                 acc = bank()
                 nc.tensor.matmul_mx(
                     out=acc[:],
-                    lhsT=w3q[a][0][:, P * t : P * (t + 1)].bitcast(FP8X4),
-                    lhsT_scale=w3q[a][1][:, P * t : P * (t + 1)],
-                    rhs=eq[hh][0][:].bitcast(FP8X4),
-                    rhs_scale=eq[hh][1][:],
+                    lhsT=w3_mx[a][0][:, P * t : P * (t + 1)].bitcast(FP8X4),
+                    lhsT_scale=w3_mx[a][1][:, P * t : P * (t + 1)],
+                    rhs=e_mx[hh][0][:].bitcast(FP8X4),
+                    rhs_scale=e_mx[hh][1][:],
                     start=True, stop=True,
                 )
-                nc.scalar.copy(h[:, HALF * hh : HALF * (hh + 1)], acc[:])
+                nc.scalar.copy(h[:, half(hh)], acc[:])
                 accs.append(acc)
-            if k == 0:
-                nc.vector.tensor_scalar(page[:], h[:], rows["shade0"][:, col], None, ALU.add)
-            else:
-                for hh in range(2):
-                    nc.scalar.activation(
-                        page[:, HALF * hh : HALF * (hh + 1)], accs[hh][:], ACT.Identity, bias=rows["shade0"][:, col]
-                    )
-            look = ring.tile([P, LOOKS], F32, name="look", tag="look", bufs=3)
+            shade = row_values["shade0"][:, col]
+            for hh in range(2):
+                if k == 0:
+                    nc.vector.tensor_scalar(page[:, half(hh)], h[:, half(hh)], shade, None, ALU.add)
+                else:
+                    nc.scalar.activation(page[:, half(hh)], accs[hh][:], ACT.Identity, bias=shade)
+            look = ring.tile([P, LOOKS], F32, name="look", tag="look", bufs=4)
             parts = 2 if k == 0 else 1
             width = LOOKS // parts
             for part in range(parts):
                 cols = slice(width * part, width * (part + 1))
-                entries = slice(width * part // 16, width * (part + 1) // 16)
+                entries = slice(width * part // PER_COLUMN, width * (part + 1) // PER_COLUMN)
                 nc.scalar.activation(
                     out=look[:, cols], in_=h[:].indirect(pos1_sb[:, entries]), func=ACT.Sigmoid,
-                    bias=rows["thr"][:, col], scale=rows["slope"][:, col],
+                    bias=row_values["thr"][:, col], scale=row_values["slope"][:, col],
                 )
-                if k == 0:
-                    nc.vector.tensor_tensor(look[:, cols], look[:, cols], slot(k)[:, cols], ALU.mult)
-                else:
-                    nc.gpsimd.tensor_tensor(look[:, cols], look[:, cols], slot(k)[:, cols], ALU.mult)
-                nc.vector.tensor_copy(page[:].indirect(pos2_sb[:, entries]), look[:, cols])
+                if part == 0:
+                    nc.vector.tensor_tensor(tint_of(k), tint_of(k), wgs_sb[:, t, :], ALU.mult)
+                nc.vector.tensor_tensor(
+                    page[:].indirect(pos2_sb[:, entries]), look[:, cols], tint_of(k)[:, cols], ALU.mult
+                )
             pages[k] = page
 
         def round_page(k):
             a, t = divmod(k, PACK)
-            nc.gpsimd.tensor_scalar(
-                slot(k + 1).bitcast(BF16), pages[k][:], rows["gain2"][:, k : k + 1], 0.0, ALU.mult, ALU.add
-            )
+            factor = row_values["gain2"][:, k : k + 1]
+            if k in ROUNDED_ON_VECTOR:
+                nc.vector.tensor_scalar(y_plain[a][:, t, :], pages[k][:], factor, None, ALU.mult)
+            else:
+                nc.scalar.activation(y_plain[a][:, t, :], pages[k][:], ACT.Copy, scale=factor)
 
-        def multiply(a, codes, scales, j0, width):
-            hh, lo = divmod(j0, HALF)
+        out_banks = {}
+        y_mx_first = []
+
+        def readout_pass(a, hh, codes, scales):
             for c in range(N // P):
                 nc.tensor.matmul_mx(
-                    out=outs[hh, c][:, lo : lo + width],
-                    lhsT=w4w[:, a, P * c : P * (c + 1)].bitcast(FP8X4),
-                    lhsT_scale=w4s[:, a, P * c : P * (c + 1)],
-                    rhs=codes.bitcast(FP8X4),
-                    rhs_scale=scales,
+                    out=out_banks[hh, c][:],
+                    lhsT=w4_word_sb[:, a, P * c : P * (c + 1)].bitcast(FP8X4),
+                    lhsT_scale=w4_scale_sb[:, a, P * c : P * (c + 1)],
+                    rhs=codes[:].bitcast(FP8X4),
+                    rhs_scale=scales[:],
                     start=(a == 0), stop=(a == 1),
                 )
 
-        yq0 = []
+        groups = HALF // PACK
 
-        def weave_first(hh):
+        def quantise_first_rows(hh):
             woven = staged()
-            nc.scalar.copy(*interleave_views(yplain[0], slice(HALF * hh, HALF * (hh + 1)), woven))
-            yq0.append(quantise(woven, "yq0%d" % hh))
+            dst, src = weave_views(y_plain[0], half(hh), woven)
+            for c0 in (0, groups // 2):
+                nc.scalar.copy(dst[:, c0 : c0 + groups // 2], src[:, c0 : c0 + groups // 2])
+            y_mx_first.append(quantise(woven, "y_mx0%d" % hh))
 
-        def first_block():
-            for hh in range(2):
-                codes, scales = yq0[hh]
-                for c in range(N // P):
-                    outs[hh, c] = bank()
-                multiply(0, codes[:], scales[:], HALF * hh, HALF)
-
-        def last_block():
-            k = H // P - 1
-            gcol = rows["gain2"][:, k : k + 1]
-            nc.vector.tensor_scalar(yplain[1][:, PACK - 1, 0:HALF], pages[k][:, 0:HALF], gcol, None, ALU.mult)
-            nc.scalar.activation(yplain[1][:, PACK - 1, HALF:S], pages[k][:, HALF:S], ACT.Copy, scale=gcol)
-            woven = [staged(), staged()]
-            nc.vector.tensor_copy(*interleave_views(yplain[1], slice(0, HALF), woven[0]))
-            out_s, in_s = interleave_views(yplain[1], slice(HALF, S), woven[1])
-            nc.scalar.copy(out_s[:, 0:64], in_s[:, 0:64])
-            for hh in range(2):
-                if hh == 1:
-                    nc.vector.tensor_copy(out_s[:, 64:128], in_s[:, 64:128])
-                codes, scales = quantise(woven[hh], "yq1%d" % hh)
-                multiply(1, codes[:], scales[:], HALF * hh, HALF)
-                for c in range(N // P):
-                    res = ring.tile([P, HALF], F32, name="res", tag="res", bufs=8)
-                    if hh == 0 or c % 2 == 0:
-                        nc.scalar.activation(res[:], outs[hh, c][:], ACT.Copy, scale=tone_sb[:, c : c + 1])
-                    else:
-                        nc.vector.tensor_scalar(res[:], outs[hh, c][:], tone_sb[:, c : c + 1], None, ALU.mult)
-                    nc.sync.dma_start(out[P * c : P * (c + 1), HALF * hh : HALF * (hh + 1)], res[:])
-
-        tiles = H // P
-        for t in range(PACK):
-            nc.vector.tensor_tensor(slot(t), slot(t), wgs_sb[:, t, :], ALU.mult)
-        for t in range(PACK):
-            nc.gpsimd.tensor_tensor(slot(PACK + t), slot(PACK + t), wgs_sb[:, t, :], ALU.mult)
-        for k in range(tiles):
+        for k in range(ROW_TILES):
             look_and_put(k)
             if k == 0:
-                prepare_w3(1)
-            if k >= 1:
-                round_page(k - 1)
-        weave_first(0)
-        weave_first(1)
-        first_block()
-        last_block()
+                quantise_rest_of_w3()
+            if k >= 2:
+                round_page(k - 2)
+            if k - 2 in (PACK - 1, PACK):
+                quantise_first_rows(k - 2 - (PACK - 1))
+        round_page(ROW_TILES - 2)
+
+        for hh in range(2):
+            for c in range(N // P):
+                out_banks[hh, c] = bank()
+            readout_pass(0, hh, *y_mx_first[hh])
+
+        last = ROW_TILES - 1
+        factor = row_values["gain2"][:, last : last + 1]
+        nc.vector.tensor_scalar(y_plain[1][:, PACK - 1, half(0)], pages[last][:, half(0)], factor, None, ALU.mult)
+        nc.scalar.activation(y_plain[1][:, PACK - 1, half(1)], pages[last][:, half(1)], ACT.Copy, scale=factor)
+        y_woven = [staged(), staged()]
+        nc.vector.tensor_copy(*weave_views(y_plain[1], half(0), y_woven[0]))
+        dst, src = weave_views(y_plain[1], half(1), y_woven[1])
+        nc.scalar.copy(dst[:, 0 : groups // 2], src[:, 0 : groups // 2])
+        for hh in range(2):
+            if hh == 1:
+                nc.vector.tensor_copy(dst[:, groups // 2 : groups], src[:, groups // 2 : groups])
+            readout_pass(1, hh, *quantise(y_woven[hh], "y_mx1%d" % hh))
+            for c in range(N // P):
+                result = joined[hh, c]
+                if hh == 0 or c % 2 == 0:
+                    nc.scalar.activation(result[:], out_banks[hh, c][:], ACT.Copy, scale=tone_sb[:, c : c + 1])
+                else:
+                    nc.vector.tensor_scalar(result[:], out_banks[hh, c][:], tone_sb[:, c : c + 1], None, ALU.mult)
+                nc.sync.dma_start(out[P * c : P * (c + 1), half(hh)], result[:])

from contextlib import ExitStack

import concourse.mybir as mybir

K, T, S, LOOKS, M, H, N = 1024, 2048, 1024, 512, 512, 1024, 512
FLOPS = 2 * (2 * K * M * S + M * H * S + H * N * S)

F32 = mybir.dt.float32
BF16 = mybir.dt.bfloat16
I32 = mybir.dt.int32
U32 = mybir.dt.uint32
U16 = mybir.dt.uint16
U8 = mybir.dt.uint8
FP8X4 = mybir.dt.float8_e4m3fn_x4
FP4X4 = mybir.dt.float4_e2m1fn_x4
ACT = mybir.ActivationFunctionType
ALU = mybir.AluOpType

P = 128
PACK = 4
KP = P * PACK
HALF = 512
QUAD = 32
QUADS = P // QUAD
PER_COLUMN = 16
ROW_TILES = H // P
ROUNDED_ON_VECTOR = (1, 3)


def tile_list_indigo_shade_readout_kernel(
    tc, tab_words, tab_scales, offs, pos1, pos2, w1_words, w1_scales, w2, gain, w3,
    slope, thr, tint, shade0, wgs, gain2, w4_words, w4_scales, tone, out,
):
    nc = tc.nc
    with ExitStack() as ctx:
        keep = ctx.enter_context(tc.tile_pool(name="keep", bufs=1))
        ring = ctx.enter_context(tc.tile_pool(name="ring", bufs=1))
        psum = ctx.enter_context(tc.psum_pool(name="psum", bufs=8))

        def held(shape, dtype, name):
            return keep.tile(shape, dtype, name=name, align_bytes=64)

        def staged():
            return ring.tile([P, PACK * HALF], BF16, name="staged", tag="staged", bufs=8, align_bytes=64)

        def row_tile():
            return ring.tile([P, S], F32, name="row_tile", tag="row_tile", bufs=6)

        def bank():
            return psum.tile([P, HALF], F32, name="bank", tag="bank")

        def half(hh):
            return slice(HALF * hh, HALF * (hh + 1))

        offs_sb = held([P, S // PER_COLUMN], U16, "offs_sb")
        pos1_sb = held([P, LOOKS // PER_COLUMN], U16, "pos1_sb")
        pos2_sb = held([P, LOOKS // PER_COLUMN], U16, "pos2_sb")
        tab_scale_sb = held([P, T], U8, "tab_scale_sb")
        w1_scale_raw = held([P, 2, M], U8, "w1_scale_raw")
        picked_scales = [held([P, S], U8, "picked_scales0"), held([P, S], U8, "picked_scales1")]
        w4_scale_sb = held([P, 2, N], U8, "w4_scale_sb")
        nc.vector.memset(tab_scale_sb[:].bitcast(I32), 0)
        nc.vector.memset(w1_scale_raw[:].bitcast(I32), 0)
        nc.vector.memset(picked_scales[1][:].bitcast(I32), 0)
        nc.vector.memset(w4_scale_sb[:].bitcast(I32), 0)

        tab_word_sb = [held([P, T], U32, "tab_word_sb%d" % a) for a in range(2)]
        w1_word_raw = held([P, 2, 2 * M], U8, "w1_word_raw")
        w2_raw = [held([P, PACK, M], F32, "w2_raw%d" % a) for a in range(2)]
        w3_raw = [held([P, PACK, KP], F32, "w3_raw%d" % a) for a in range(2)]
        gain_sb = held([P, PACK], F32, "gain_sb")
        wgs_sb = held([P, PACK, LOOKS], F32, "wgs_sb")
        tint_sb = held([P, ROW_TILES * LOOKS], F32, "tint_sb")
        w4_word_sb = held([P, 2, N], U32, "w4_word_sb")
        tone_sb = held([P, N // P], F32, "tone_sb")
        row_values = {}

        def tint_of(k, n=1):
            return tint_sb[:, LOOKS * k : LOOKS * (k + n)]

        def load_tab(a):
            nc.sync.dma_start(tab_word_sb[a][:].bitcast(I32), tab_words[a].rearrange("p t i -> p (t i)").bitcast(I32))

        def load_w2(a):
            nc.sync.dma_start(w2_raw[a][:], w2[KP * a : KP * (a + 1), :].rearrange("(p j) c -> p j c", j=PACK))

        def load_w3(a):
            nc.sync.dma_start(w3_raw[a][:], w3[:, KP * a : KP * (a + 1)].rearrange("(p j) c -> p j c", j=PACK))

        def load_tint(k, n):
            a, t = divmod(k, PACK)
            four_rows = tint[KP * a : KP * (a + 1), :].rearrange("(p i) j -> p (i j)", i=PACK)
            nc.sync.dma_start(tint_of(k, n), four_rows[:, LOOKS * t : LOOKS * (t + n)])

        def load_row_values(name, vec):
            row_values[name] = held([P, ROW_TILES], F32, name + "_sb")
            nc.sync.dma_start(
                row_values[name][:].rearrange("p (a i) -> p a i", i=PACK), vec.rearrange("(a p i) -> p a i", a=2, i=PACK)
            )

        def load_scale_rows(dst, src, q):
            nc.sync.dma_start(
                dst[QUAD * q : QUAD * q + 4, :, :].bitcast(I32),
                src[:, 4 * q : 4 * q + 4, :].rearrange("a r c -> r a c").bitcast(I32),
            )

        nc.sync.dma_start(offs_sb[:], offs)
        nc.sync.dma_start(w1_word_raw[:].bitcast(I32), w1_words.rearrange("a p c -> p a c").bitcast(I32))
        for q in range(QUADS):
            nc.sync.dma_start(
                tab_scale_sb[QUAD * q : QUAD * q + 8, :].bitcast(I32), tab_scales[:, 4 * q : 4 * q + 4, :].bitcast(I32)
            )
        load_tab(0)
        for q in range(QUADS):
            load_scale_rows(w1_scale_raw, w1_scales, q)
        load_w2(0)
        load_tab(1)
        load_w2(1)
        nc.sync.dma_start(gain_sb[:], gain.rearrange("(p i) -> p i", i=PACK))
        load_w3(0)
        nc.sync.dma_start(pos1_sb[:], pos1)
        load_row_values("slope", slope)
        load_w3(1)
        load_row_values("thr", thr)
        load_row_values("shade0", shade0)
        for q in range(QUADS):
            nc.sync.dma_start(wgs_sb[QUAD * q : QUAD * (q + 1), :, :], wgs.rearrange("(p i) j -> p i j", i=PACK))
        load_tint(0, 2)
        nc.sync.dma_start(pos2_sb[:], pos2)
        load_tint(2, 2)
        load_row_values("gain2", gain2)
        load_tint(PACK, PACK)
        nc.sync.dma_start(w4_word_sb[:].bitcast(I32), w4_words.rearrange("a p c i -> p a (c i)").bitcast(I32))
        for q in range(QUADS):
            load_scale_rows(w4_scale_sb, w4_scales, q)
        with nc.allow_non_contiguous_dma(reason="one value a partition"):
            nc.sync.dma_start(tone_sb[:], tone.rearrange("(c p) -> p c", p=P))

        nc.vector.tensor_copy(picked_scales[0][:], tab_scale_sb[:].indirect(offs_sb[:]))
        span = QUAD * (QUADS - 1) + 4
        nc.scalar.dma_start(picked_scales[1][0:span, :].bitcast(I32), picked_scales[0][4 : 4 + span, :].bitcast(I32))

        picked_words = [[held([P, HALF], U32, "picked_words%d%d" % (a, hh)) for hh in range(2)] for a in range(2)]

        def gather_words(a, hh):
            entries = slice(HALF // PER_COLUMN * hh, HALF // PER_COLUMN * (hh + 1))
            nc.vector.tensor_copy(picked_words[a][hh][:], tab_word_sb[a][:].indirect(offs_sb[:, entries]))

        gather_words(0, 0)
        w1_word_sb = held([P, 2, 2 * M], U8, "w1_word_sb")
        w1_scale_sb = held([P, 2, M], U8, "w1_scale_sb")
        nc.vector.tensor_copy(
            w1_word_sb[:].bitcast(U16).rearrange("p a (t q) -> p a t q", t=PACK),
            w1_word_raw[:].bitcast(U16).rearrange("p a (q t) -> p a t q", t=PACK),
        )
        nc.vector.tensor_copy(
            w1_scale_sb[:].rearrange("p a (t q) -> p a t q", t=PACK),
            w1_scale_raw[:].rearrange("p a (q t) -> p a t q", t=PACK),
        )
        gather_words(0, 1)
        gather_words(1, 0)
        gather_words(1, 1)

        def deal_views(raw, dst, q0, q1):
            return (
                dst[:].rearrange("p (t q j) -> p q j t", t=PACK, j=PACK)[:, q0:q1],
                raw[:].rearrange("p j (q t) -> p q j t", t=PACK)[:, q0:q1],
            )

        def quantise(src, name):
            codes = held([P, HALF], U32, name + "_codes")
            scales = held([P, HALF], U8, name + "_scales")
            nc.vector.quantize_mx(out=codes[:].bitcast(FP8X4), scales=scales[:], in_=src[:])
            return codes, scales

        w2_bf = [staged(), staged()]
        nc.vector.tensor_copy(*deal_views(w2_raw[0], w2_bf[0], 0, P))
        nc.scalar.copy(*deal_views(w2_raw[1], w2_bf[1], 0, P // 2))
        w2_mx = [quantise(w2_bf[0], "w2_mx0")]
        nc.vector.tensor_copy(*deal_views(w2_raw[1], w2_bf[1], P // 2, P))
        w2_mx.append(quantise(w2_bf[1], "w2_mx1"))

        joined = {}
        w1_banks = {(hh, i): bank() for hh in range(2) for i in range(PACK)}
        for a in range(2):
            for hh in range(2):
                for i in range(PACK):
                    nc.tensor.matmul_mx(
                        out=w1_banks[hh, i][:],
                        lhsT=w1_word_sb[:, a, 2 * P * i : 2 * P * (i + 1)].bitcast(FP4X4),
                        lhsT_scale=w1_scale_sb[:, a, P * i : P * (i + 1)],
                        rhs=picked_words[a][hh][:].bitcast(FP8X4),
                        rhs_scale=picked_scales[a][:, half(hh)],
                        start=(a == 0), stop=(a == 1),
                    )
                    if a == 1:
                        joined[hh, i] = held([P, HALF], F32, "joined%d%d" % (hh, i))
                        nc.scalar.copy(joined[hh, i][:], w1_banks[hh, i][:])

        def weave_views(plain, cols, dst):
            return (
                dst[:].rearrange("p (c i t) -> p c t i", i=PACK, t=PACK),
                plain[:, :, cols].rearrange("p t (c i) -> p c t i", i=PACK),
            )

        e_plain = []
        for hh in range(2):
            e_plain.append(staged()[:].rearrange("p (t c) -> p t c", t=PACK))
            for i in range(PACK):
                acc = bank()
                for a in range(2):
                    nc.tensor.matmul_mx(
                        out=acc[:],
                        lhsT=w2_mx[a][0][:, P * i : P * (i + 1)].bitcast(FP8X4),
                        lhsT_scale=w2_mx[a][1][:, P * i : P * (i + 1)],
                        rhs=picked_words[a][hh][:].bitcast(FP8X4),
                        rhs_scale=picked_scales[a][:, half(hh)],
                        start=(a == 0), stop=(a == 1),
                    )
                nc.vector.tensor_tensor(joined[hh, i][:], acc[:], joined[hh, i][:], ALU.max)
                nc.gpsimd.tensor_scalar(
                    e_plain[hh][:, i, :], joined[hh, i][:], gain_sb[:, i : i + 1], 0.0, ALU.mult, ALU.add
                )

        e_woven = [staged(), staged()]
        nc.scalar.copy(*weave_views(e_plain[0], half(0), e_woven[0]))
        e_mx = [quantise(e_woven[0], "e_mx0")]
        nc.vector.tensor_copy(*weave_views(e_plain[1], half(0), e_woven[1]))
        e_mx.append(quantise(e_woven[1], "e_mx1"))

        w3_bf = staged()
        for q0 in range(0, P, P // 4):
            nc.scalar.copy(*deal_views(w3_raw[0], w3_bf, q0, q0 + P // 4))
        w3_mx = [quantise(w3_bf, "w3_mx0")]

        def quantise_rest_of_w3():
            rest_bf = staged()
            nc.vector.tensor_copy(*deal_views(w3_raw[1], rest_bf, 0, P))
            w3_mx.append(quantise(rest_bf, "w3_mx1"))

        h_tiles = {}
        pages = {}
        y_plain = [held([P, PACK, S], BF16, "y_plain%d" % a) for a in range(2)]

        def look_and_put(k):
            a, t = divmod(k, PACK)
            col = slice(k, k + 1)
            h = row_tile()
            h_tiles[k] = h
            page = row_tile() if k == 0 else h_tiles[k - 1]
            accs = []
            for hh in range(2):
                acc = bank()
                nc.tensor.matmul_mx(
                    out=acc[:],
                    lhsT=w3_mx[a][0][:, P * t : P * (t + 1)].bitcast(FP8X4),
                    lhsT_scale=w3_mx[a][1][:, P * t : P * (t + 1)],
                    rhs=e_mx[hh][0][:].bitcast(FP8X4),
                    rhs_scale=e_mx[hh][1][:],
                    start=True, stop=True,
                )
                nc.scalar.copy(h[:, half(hh)], acc[:])
                accs.append(acc)
            shade = row_values["shade0"][:, col]
            for hh in range(2):
                if k == 0:
                    nc.vector.tensor_scalar(page[:, half(hh)], h[:, half(hh)], shade, None, ALU.add)
                else:
                    nc.scalar.activation(page[:, half(hh)], accs[hh][:], ACT.Identity, bias=shade)
            look = ring.tile([P, LOOKS], F32, name="look", tag="look", bufs=4)
            parts = 2 if k == 0 else 1
            width = LOOKS // parts
            for part in range(parts):
                cols = slice(width * part, width * (part + 1))
                entries = slice(width * part // PER_COLUMN, width * (part + 1) // PER_COLUMN)
                nc.scalar.activation(
                    out=look[:, cols], in_=h[:].indirect(pos1_sb[:, entries]), func=ACT.Sigmoid,
                    bias=row_values["thr"][:, col], scale=row_values["slope"][:, col],
                )
                if part == 0:
                    nc.vector.tensor_tensor(tint_of(k), tint_of(k), wgs_sb[:, t, :], ALU.mult)
                nc.vector.tensor_tensor(
                    page[:].indirect(pos2_sb[:, entries]), look[:, cols], tint_of(k)[:, cols], ALU.mult
                )
            pages[k] = page

        def round_page(k):
            a, t = divmod(k, PACK)
            factor = row_values["gain2"][:, k : k + 1]
            if k in ROUNDED_ON_VECTOR:
                nc.vector.tensor_scalar(y_plain[a][:, t, :], pages[k][:], factor, None, ALU.mult)
            else:
                nc.scalar.activation(y_plain[a][:, t, :], pages[k][:], ACT.Copy, scale=factor)

        out_banks = {}
        y_mx_first = []

        def readout_pass(a, hh, codes, scales):
            for c in range(N // P):
                nc.tensor.matmul_mx(
                    out=out_banks[hh, c][:],
                    lhsT=w4_word_sb[:, a, P * c : P * (c + 1)].bitcast(FP8X4),
                    lhsT_scale=w4_scale_sb[:, a, P * c : P * (c + 1)],
                    rhs=codes[:].bitcast(FP8X4),
                    rhs_scale=scales[:],
                    start=(a == 0), stop=(a == 1),
                )

        groups = HALF // PACK

        def quantise_first_rows(hh):
            woven = staged()
            dst, src = weave_views(y_plain[0], half(hh), woven)
            for c0 in (0, groups // 2):
                nc.scalar.copy(dst[:, c0 : c0 + groups // 2], src[:, c0 : c0 + groups // 2])
            y_mx_first.append(quantise(woven, "y_mx0%d" % hh))

        for k in range(ROW_TILES):
            look_and_put(k)
            if k == 0:
                quantise_rest_of_w3()
            if k >= 2:
                round_page(k - 2)
            if k - 2 in (PACK - 1, PACK):
                quantise_first_rows(k - 2 - (PACK - 1))
        round_page(ROW_TILES - 2)

        for hh in range(2):
            for c in range(N // P):
                out_banks[hh, c] = bank()
            readout_pass(0, hh, *y_mx_first[hh])

        last = ROW_TILES - 1
        factor = row_values["gain2"][:, last : last + 1]
        nc.vector.tensor_scalar(y_plain[1][:, PACK - 1, half(0)], pages[last][:, half(0)], factor, None, ALU.mult)
        nc.scalar.activation(y_plain[1][:, PACK - 1, half(1)], pages[last][:, half(1)], ACT.Copy, scale=factor)
        y_woven = [staged(), staged()]
        nc.vector.tensor_copy(*weave_views(y_plain[1], half(0), y_woven[0]))
        dst, src = weave_views(y_plain[1], half(1), y_woven[1])
        nc.scalar.copy(dst[:, 0 : groups // 2], src[:, 0 : groups // 2])
        for hh in range(2):
            if hh == 1:
                nc.vector.tensor_copy(dst[:, groups // 2 : groups], src[:, groups // 2 : groups])
            readout_pass(1, hh, *quantise(y_woven[hh], "y_mx1%d" % hh))
            for c in range(N // P):
                result = joined[hh, c]
                if hh == 0 or c % 2 == 0:
                    nc.scalar.activation(result[:], out_banks[hh, c][:], ACT.Copy, scale=tone_sb[:, c : c + 1])
                else:
                    nc.vector.tensor_scalar(result[:], out_banks[hh, c][:], tone_sb[:, c : c + 1], None, ALU.mult)
                nc.sync.dma_start(out[P * c : P * (c + 1), half(hh)], result[:])
